import numpy as np
import ml_dtypes


def mxq(x, axis, fmt="e4m3"):
    dtype, down = {"e4m3": (ml_dtypes.float8_e4m3fn, 7), "e5m2": (ml_dtypes.float8_e5m2, 14)}[fmt]
    v = np.moveaxis(np.asarray(x, np.float32).astype(ml_dtypes.bfloat16).astype(np.float64), axis, -1)
    blocks = v.reshape(v.shape[:-1] + (-1, 32))
    amax = np.abs(blocks).max(-1, keepdims=True)
    byte = np.maximum(np.where(amax > 0, np.frexp(amax)[1] - 1 + 127, 0) - down, 1)
    scale = np.exp2(byte - 127.0)
    codes = (blocks / scale).astype(np.float32).astype(dtype).astype(np.float64)
    return np.moveaxis((codes * scale).reshape(v.shape), -1, axis)


WIDE = False


def mx_kscale(k):
    if not WIDE:
        return np.ones(k)
    levels = np.array([24, -24, 12, -12, 0])
    if k % 512:
        return np.exp2(np.random.permutation(np.resize(levels, k // 32))).repeat(32)
    a = np.empty((k // 512, 16))
    for p in range(k // 512):
        a[p, :8] = np.random.permutation(np.resize(levels, 8))
        for g in range(8):
            far = levels[np.abs(levels - a[p, g]) >= 10]
            a[p, g + 8] = far[np.random.randint(len(far))]
    return np.exp2(a.ravel()).repeat(32)


def f64(x):
    return np.asarray(x).astype(np.float64)


E2M1 = np.array([0.0, 0.5, 1.0, 1.5, 2.0, 3.0, 4.0, 6.0, -0.0, -0.5, -1.0, -1.5, -2.0, -3.0, -4.0, -6.0])


def pack_weight(w, fmt):
    k, n = w.shape
    w = f64(np.asarray(w, np.float32).astype(ml_dtypes.bfloat16)).reshape(k // 32, 32, n)
    amax = np.abs(w).max(1)
    if fmt == "e4m3":
        byte = np.frexp(amax)[1] - 1 + 127 - 7
    else:
        mant, ex = np.frexp(amax / 6.0)
        byte = np.where(mant > 0.5, ex, ex - 1) + 127
    byte = np.clip(np.where(amax > 0, byte, 1), 1, 254)
    scaled = (w * np.exp2(127.0 - byte)[:, None, :]).reshape(k, n).astype(np.float32)
    by_word = np.ascontiguousarray(scaled.reshape(k // 512, 128, 4, n).transpose(0, 1, 3, 2))
    if fmt == "e4m3":
        words = by_word.astype(ml_dtypes.float8_e4m3fn).view(np.uint8)
    else:
        c = by_word.astype(ml_dtypes.float4_e2m1fn).view(np.uint8) & 0xF
        words = (c[..., 0::2] | (c[..., 1::2] << 4)).reshape(k // 512, 128, 2 * n)
    return np.ascontiguousarray(words), np.ascontiguousarray(byte.astype(np.uint8).reshape(k // 512, 16, n))


def unpack_weight(words, scales, fmt):
    g, _, n = scales.shape
    words = np.ascontiguousarray(words).reshape(g, 128, n, -1)
    if fmt == "e4m3":
        vals = words.view(ml_dtypes.float8_e4m3fn).astype(np.float64)
    else:
        nib = np.empty((g, 128, n, 4), np.uint8)
        nib[..., 0::2] = words & 0xF
        nib[..., 1::2] = words >> 4
        vals = E2M1[nib]
    vals = vals * np.repeat(np.exp2(scales.astype(np.float64) - 127.0), 8, axis=1)[..., None]
    return vals.transpose(0, 1, 3, 2).reshape(g * 512, n)


K, F, N, T = 512, 1024, 128, 1024


def setup_inputs():
    n = np.random.standard_normal
    s = mx_kscale(K)[:, None]
    u = mx_kscale(F)[:, None]
    p_fb = pack_weight(np.abs(n((F, N))) / F / u, "e2m1")
    return {
        "x": (n((K, T)) * s).astype(np.float32),
        "co": (n((K, F)) / np.sqrt(K) / s).astype(np.float32),
        "si": (n((K, F)) / np.sqrt(K) / s).astype(np.float32),
        "gn": (np.random.uniform(0.5, 2.0, F) * u[:, 0]).astype(np.float32),
        "fb_words": p_fb[0],
        "fb_scales": p_fb[1],
        "mu": (np.random.uniform(0.5, 1.5, N)).astype(np.float32),
        "isd": (np.random.uniform(0.5, 2.0, N)).astype(np.float32),
    }


def reference(x, co, si, gn, fb_words, fb_scales, mu, isd):
    x_ = mxq(f64(x), 0, "e4m3")
    co_ = mxq(f64(co), 0, "e4m3")
    si_ = mxq(f64(si), 0, "e4m3")
    re = co_.T @ x_
    im = si_.T @ x_
    h = f64(gn)[:, None] * ((re) ** 2 + (im) ** 2)
    h_ = mxq(h, 0, "e4m3")
    fb_ = unpack_weight(fb_words, fb_scales, "e2m1")
    y = fb_.T @ h_
    return (y - f64(mu)[:, None]) * f64(isd)[:, None]

@@ -1,0 +1,323 @@
+from contextlib import ExitStack
+
+import concourse.mybir as mybir
+from concourse.masks import make_identity
+
+K, F, N, T = 512, 1024, 128, 1024
+FLOPS = 2 * 2 * K * F * T + 2 * F * N * T
+
+F32 = mybir.dt.float32
+BF16 = mybir.dt.bfloat16
+U32 = mybir.dt.uint32
+I32 = mybir.dt.int32
+U8 = mybir.dt.uint8
+FP8X4 = mybir.dt.float8_e4m3fn_x4
+FP4X4 = mybir.dt.float4_e2m1fn_x4
+ALU = mybir.AluOpType
+ACT = mybir.ActivationFunctionType
+
+P = 128
+PACK = 4
+HALF = 512
+
+
+def tile_mix_mel_norm_kernel(tc, x, co, si, gn, fb_words, fb_scales, mu, isd, out):
+    nc = tc.nc
+    with ExitStack() as ctx:
+        keep = ctx.enter_context(tc.tile_pool(name="keep", bufs=1))
+        work = ctx.enter_context(tc.tile_pool(name="work", bufs=1))
+        psum = ctx.enter_context(tc.psum_pool(name="psum", bufs=1))
+        ctx.enter_context(tc.manual_schedule())
+
+        gain = keep.tile([P, 2, PACK], F32, name="gain")
+        nc.scalar.dma_start(out=gain[:], in_=gn.rearrange("(a p j) -> p a j", a=2, j=PACK))
+
+        def load(src, c0, width, name):
+            raw = keep.tile([P, PACK, width], F32, name=name, align_bytes=64)
+            nc.sync.dma_start(out=raw[:], in_=src[:, c0 : c0 + width].rearrange("(p j) w -> p j w", j=PACK))
+            return raw
+
+        raw = {}
+        for name, c in (("x", 0), ("co", 0), ("x", 1), ("co", 1), ("si", 0), ("si", 1), ("x", 2), ("co", 2), ("x", 3), ("co", 3), ("si", 2), ("si", 3)):
+            raw[(name, c)] = load({"x": x, "co": co, "si": si}[name], 256 * c, 256, "%s%d" % (name, c))
+
+        warm = keep.tile([P, 1], F32, name="warm")
+        nc.vector.memset(warm[:], 0.0)
+        warm_out = keep.tile([P, 1], F32, name="warm_out")
+        nc.scalar.activation(out=warm_out[:], in_=warm[:], func=ACT.Square)
+
+        fb_scale = keep.tile([P, 2, N], U8, name="fb_scale", align_bytes=64)
+        nc.gpsimd.memset(fb_scale[:].bitcast(I32), 0)
+        ident = keep.tile([P, P], F32, name="ident", align_bytes=64)
+        half = keep.tile([P, PACK], F32, name="half")
+        nc.gpsimd.memset(half[:], 0.5)
+        make_identity(nc, ident[:])
+
+        is_pos = keep.tile([P, PACK], F32, name="is_pos")
+        nc.gpsimd.tensor_scalar(out=is_pos[:], in0=gain[:, 1, :], scalar1=0.0, scalar2=2.0, op0=ALU.is_ge, op1=ALU.mult)
+        sgn = keep.tile([P, PACK], F32, name="sgn")
+        nc.gpsimd.tensor_scalar(out=sgn[:], in0=is_pos[:], scalar1=1.0, scalar2=-1.0, op0=ALU.mult, op1=ALU.add)
+        mag = keep.tile([P, PACK], F32, name="mag")
+        nc.gpsimd.tensor_tensor(out=mag[:], in0=gain[:, 1, :], in1=sgn[:], op=ALU.mult)
+        root = keep.tile([P, PACK], F32, name="root")
+        nc.gpsimd.tensor_tensor(out=root[:], in0=mag[:], in1=half[:], op=ALU.pow)
+        sgn_rep = keep.tile([P, 16, PACK], BF16, name="sgn_rep", align_bytes=64)
+        nc.gpsimd.tensor_copy(out=sgn_rep[:], in_=sgn[:].unsqueeze(1).to_broadcast([P, 16, PACK]))
+
+        fb_code = keep.tile([P, 2, 2 * N], U8, name="fb_code", align_bytes=64)
+        nc.sync.dma_start(out=fb_code[:], in_=fb_words.rearrange("a p b -> p a b"))
+        scale_rows = fb_scales.rearrange("a (q r) n -> r q a n", r=4)
+        for r in range(4):
+            nc.sync.dma_start(out=fb_scale[r:P:32].bitcast(I32), in_=scale_rows[r].bitcast(I32))
+        mean = keep.tile([P, 1], F32, name="mean")
+        nc.sync.dma_start(out=mean[:], in_=mu.rearrange("(p o) -> p o", o=1))
+        inv_dev = keep.tile([P, 1], F32, name="inv_dev")
+        nc.sync.dma_start(out=inv_dev[:], in_=isd.rearrange("(p o) -> p o", o=1))
+        shift = keep.tile([P, 1], F32, name="shift")
+        nc.gpsimd.tensor_scalar(out=shift[:], in0=mean[:], scalar1=inv_dev[:], scalar2=-1.0, op0=ALU.mult, op1=ALU.mult)
+
+        x_code = keep.tile([P, T], U32, name="x_code", align_bytes=64)
+        x_scale = keep.tile([P, T], U8, name="x_scale", align_bytes=64)
+        w_code = [[keep.tile([P, HALF], U32, name="wc%d%d" % (s, a), align_bytes=64) for a in range(2)] for s in range(2)]
+        w_scale = [[keep.tile([P, HALF], U8, name="ws%d%d" % (s, a), align_bytes=64) for a in range(2)] for s in range(2)]
+        h_code = [keep.tile([P, T], U32, name="hc%d" % a, align_bytes=64) for a in range(2)]
+        h_scale = [keep.tile([P, T], U8, name="hs%d" % a, align_bytes=64) for a in range(2)]
+
+        def copy_on(engine, dst, src):
+            if engine == "v":
+                nc.vector.tensor_copy(out=dst, in_=src)
+            else:
+                nc.scalar.copy(out=dst, in_=src)
+
+        def cast(engine, raw, grouped, c0, c1):
+            dst = grouped[:].rearrange("p (w k) -> p w k", k=PACK)[:, c0:c1, :].rearrange("p (c i) k -> p c k i", i=4)
+            src = raw[:, :, c0:c1].rearrange("p k (c i) -> p c k i", i=4)
+            copy_on(engine, dst, src)
+
+        def cast_permuted(engine, src_tile, grouped, c, m0, m1):
+            dst = grouped[:].rearrange("p (j m k) -> p m k j", j=PACK, k=PACK)[:, 64 * c + m0 : 64 * c + m1]
+            src = src_tile[:].rearrange("p k (m j) -> p m k j", j=PACK)[:, m0:m1]
+            copy_on(engine, dst, src)
+
+        def grouped_tile(width, name):
+            return keep.tile([P, width * PACK], BF16, name=name, align_bytes=64)
+
+        def quantize(codes, scales, values):
+            nc.vector.quantize_mx(out=codes.bitcast(FP8X4), scales=scales, in_=values)
+
+        def mx(dst, lc, ls, rc, rs, start=True, stop=True, ldt=FP8X4):
+            nc.tensor.matmul_mx(out=dst, lhsT=lc.bitcast(ldt), lhsT_scale=ls, rhs=rc.bitcast(FP8X4), rhs_scale=rs, start=start, stop=stop)
+
+        def bank(tag, bufs):
+            return psum.tile([P, HALF], F32, name=tag, tag=tag, bufs=bufs)
+
+        sq_t = {}
+
+        def sq_tile(s):
+            return work.tile([P, 2, PACK, P], F32, name="sq%d" % s, tag="sq%d" % s, bufs=4, align_bytes=64)
+
+        def square_chunk(s, c, pair):
+            acc = bank("mm", 5)
+            fc = slice(256 * c, 256 * (c + 1))
+            for i in range(2):
+                cols = slice((2 * pair + i) * P, (2 * pair + i + 1) * P)
+                mx(acc[:, 256 * i : 256 * (i + 1)], x_code[:, cols], x_scale[:, cols], w_code[s][0][:, fc], w_scale[s][0][:, fc])
+            if c == 0:
+                sq_t[(s, 0, pair)] = sq_tile(s)
+            nc.scalar.activation(out=sq_t[(s, 0, pair)][:, :, :, 64 * c : 64 * (c + 1)], in_=acc[:].rearrange("t (i m j) -> t i j m", i=2, j=PACK), func=ACT.Square)
+
+        def square_by_frames(s, a, tt):
+            cols = slice(tt * P, (tt + 1) * P)
+            acc = bank("mm", 5)
+            mx(acc[:], x_code[:, cols], x_scale[:, cols], w_code[s][a][:], w_scale[s][a][:])
+            if tt % 2 == 0:
+                sq_t[(s, a, tt // 2)] = sq_tile(s)
+            order = "t (m j) -> t j m" if a == 0 else "t (j m) -> t j m"
+            nc.scalar.activation(out=sq_t[(s, a, tt // 2)][:, tt % 2], in_=acc[:].rearrange(order, j=PACK), func=ACT.Square)
+
+        power = {}
+
+        def transpose_add(a, tt):
+            acc = bank("tr", 3)
+            for j in range(PACK):
+                for s in range(2):
+                    nc.tensor.matmul(out=acc[:, j * P : (j + 1) * P], lhsT=sq_t[(s, a, tt // 2)][:, tt % 2, j, :], rhs=ident[:], start=(s == 0), stop=(s == 1), is_transpose=True)
+            power[(a, tt)] = acc
+
+        h_val = {}
+
+        def h_tile(key):
+            h_val[key] = work.tile([P, 256 * PACK], BF16, name="hv", tag="hv", bufs=4, align_bytes=64)
+            return h_val[key]
+
+        def apply_gain(a, tt):
+            hv = h_tile((a, tt // 2)) if tt % 2 == 0 else h_val[(a, tt // 2)]
+            i = tt % 2
+            nc.vector.tensor_tensor(
+                out=hv[:, i * HALF : (i + 1) * HALF].rearrange("p (t j) -> p t j", j=PACK),
+                in0=power[(a, tt)][:].rearrange("p (j t) -> p t j", j=PACK),
+                in1=gain[:, a, :].unsqueeze(1).to_broadcast([P, P, PACK]),
+                op=ALU.mult,
+            )
+
+        def quantize_h(a, pair):
+            cols = slice(256 * pair, 256 * (pair + 1))
+            quantize(h_code[a][:, cols], h_scale[a][:, cols], h_val[(a, pair)][:])
+
+        def quantize_h1(a, tt):
+            cols = slice(P * tt, P * (tt + 1))
+            i = tt % 2
+            quantize(h_code[a][:, cols], h_scale[a][:, cols], h_val[(a, tt // 2)][:, i * HALF : (i + 1) * HALF])
+        sq_f = {}
+
+        def square_by_freq(s, t0, width):
+            cols = slice(t0, t0 + width)
+            sq = keep.tile([P, PACK, width], F32, name="sqf%d_%d" % (s, t0), align_bytes=64)
+            per_bank = HALF // width
+            for b in range(PACK // per_bank):
+                acc = bank("mm", 5)
+                for i in range(per_bank):
+                    j = b * per_bank + i
+                    jc = slice(j * P, (j + 1) * P)
+                    mx(acc[:, i * width : (i + 1) * width], w_code[s][1][:, jc], w_scale[s][1][:, jc], x_code[:, cols], x_scale[:, cols])
+                for i in range(per_bank):
+                    j = b * per_bank + i
+                    nc.scalar.activation(out=sq[:, j, :], in_=acc[:, i * width : (i + 1) * width], func=ACT.Square, scale=root[:, j : j + 1])
+            for q in range(width // 256):
+                sq_f[(s, t0 // 256 + q)] = sq[:, :, 256 * q : 256 * (q + 1)]
+
+        h_abs = {}
+
+        def add_parts(pair):
+            ha = work.tile([P, 256 * PACK], BF16, name="ha", tag="ha", bufs=2, align_bytes=64)
+            nc.vector.tensor_tensor(
+                out=ha[:].rearrange("p (c i j) -> p c j i", i=4, j=PACK),
+                in0=sq_f[(0, pair)].rearrange("p j (c i) -> p c j i", i=4),
+                in1=sq_f[(1, pair)].rearrange("p j (c i) -> p c j i", i=4),
+                op=ALU.add,
+            )
+            h_abs[pair] = ha
+
+        def sign_parts(pair):
+            hv = h_tile((1, pair))
+            nc.vector.tensor_tensor(
+                out=hv[:].rearrange("p (r e) -> p r e", e=64),
+                in0=h_abs[pair][:].rearrange("p (r e) -> p r e", e=64),
+                in1=sgn_rep[:].rearrange("p r j -> p (r j)").unsqueeze(1).to_broadcast([P, 16, 64]),
+                op=ALU.mult,
+            )
+
+        def filter_bank(t0, width, n_cols):
+            acc = bank("mm", 5)
+            for c0 in range(0, width, n_cols):
+                cols = slice(t0 + c0, t0 + c0 + n_cols)
+                for a in range(2):
+                    mx(acc[:, c0 : c0 + n_cols], fb_code[:, a, :], fb_scale[:, a, :], h_code[a][:, cols], h_scale[a][:, cols], start=(a == 0), stop=(a == 1), ldt=FP4X4)
+            res = keep.tile([P, width], F32, name="res%d" % t0, align_bytes=64)
+            nc.scalar.activation(out=res[:], in_=acc[:, 0:width], func=ACT.Identity, scale=inv_dev[:], bias=shift[:])
+            nc.sync.dma_start(out=out[:, t0 : t0 + width], in_=res[:])
+
+        g_x = [grouped_tile(256, "g_x%d" % i) for i in range(4)]
+        g_w0 = [[grouped_tile(256, "g_w0_%d%d" % (s, c)) for c in range(2)] for s in range(2)]
+        g_w1 = [grouped_tile(HALF, "g_w1_%d" % s) for s in range(2)]
+
+        def quantize_x(i):
+            quantize(x_code[:, 256 * i : 256 * (i + 1)], x_scale[:, 256 * i : 256 * (i + 1)], g_x[i][:])
+
+        def quantize_w0(s, c):
+            quantize(w_code[s][0][:, 256 * c : 256 * (c + 1)], w_scale[s][0][:, 256 * c : 256 * (c + 1)], g_w0[s][c][:])
+
+        def quantize_w1(s):
+            quantize(w_code[s][1][:], w_scale[s][1][:], g_w1[s][:])
+
+        def warm_up(n):
+            acc = bank("tr", 3)
+            for i in range(n):
+                mx(acc[:, 0:256], x_code[:, 0:P], x_scale[:, 0:P], x_code[:, 0:256], x_scale[:, 0:256])
+
+        def sq(a, tts):
+            for tt in tts:
+                for s in range(2):
+                    square_by_frames(s, a, tt)
+        def cast_x(i):
+            cast("v", raw[("x", i)], g_x[i], 0, 256)
+        def prep_x(i):
+            cast_x(i)
+            quantize_x(i)
+        def prep_w(s, c):
+            cast("v", raw[(("co", "si")[s], c)], g_w0[s][c], 0, 256)
+            quantize_w0(s, c)
+        def cast_w1(s, c, e="v"):
+            cast_permuted(e, raw[(("co", "si")[s], 2 + c)], g_w1[s], c, 0, 64)
+        tadd = transpose_add
+        gain_ = apply_gain
+        prep_x(0)
+        warm_up(4)
+        prep_w(0, 0)
+        square_chunk(0, 0, 0)
+        warm_up(3)
+        prep_x(1)
+        square_chunk(0, 0, 1)
+        warm_up(2)
+        for s, c in ((0, 1), (1, 0), (1, 1)):
+            prep_w(s, c)
+            square_chunk(s, c, 0)
+            square_chunk(s, c, 1)
+        prep_x(2)
+        sq(0, (4, 5))
+        tadd(0, 0)
+        cast_w1(0, 0)
+        prep_x(3)
+        gain_(0, 0)
+        tadd(0, 1)
+        sq(0, (6, 7))
+        cast_w1(0, 1)
+        gain_(0, 1)
+        quantize_w1(0)
+        tadd(0, 2)
+        tadd(0, 3)
+        cast_w1(1, 0, "v")
+        quantize_h(0, 0)
+        gain_(0, 2)
+        cast_w1(1, 1)
+        square_by_freq(0, 0, 256)
+        square_by_freq(0, 256, 256)
+        gain_(0, 3)
+        quantize_w1(1)
+        tadd(0, 4)
+        tadd(0, 5)
+        quantize_h(0, 1)
+        gain_(0, 4)
+        gain_(0, 5)
+        square_by_freq(1, 0, 256)
+        square_by_freq(1, 256, 256)
+        tadd(0, 6)
+        tadd(0, 7)
+        quantize_h(0, 2)
+        add_parts(0)
+        gain_(0, 6)
+        sign_parts(0)
+        gain_(0, 7)
+        quantize_h(1, 0)
+        sq(1, (4, 5))
+        add_parts(1)
+        quantize_h(0, 3)
+        sign_parts(1)
+        sq(1, (6,))
+        tadd(1, 4)
+        sq(1, (7,))
+        tadd(1, 5)
+        gain_(1, 4)
+        quantize_h(1, 1)
+        gain_(1, 5)
+        tadd(1, 6)
+        filter_bank(0, HALF, HALF)
+        tadd(1, 7)
+        gain_(1, 6)
+        quantize_h(1, 2)
+        gain_(1, 7)
+        quantize_h1(1, 6)
+        quantize_h1(1, 7)
+        filter_bank(512, 256, P)
+        filter_bank(768, P, P)
+        filter_bank(896, P, P)

@@ -38,8 +38,10 @@ def tile_mix_mel_norm_kernel(tc, x, co, si, gn, fb_words, fb_scales, mu, isd, ou
             return raw
 
         raw = {}
-        for name, c in (("x", 0), ("co", 0), ("x", 1), ("co", 1), ("si", 0), ("si", 1), ("x", 2), ("co", 2), ("x", 3), ("co", 3), ("si", 2), ("si", 3)):
-            raw[(name, c)] = load({"x": x, "co": co, "si": si}[name], 256 * c, 256, "%s%d" % (name, c))
+        for name, c0, n in (("x", 0, 2), ("co", 0, 2), ("si", 0, 2), ("x", 2, 2), ("co", 2, 2), ("si", 2, 2)):
+            piece = load({"x": x, "co": co, "si": si}[name], 256 * c0, 256 * n, "%s%d" % (name, c0))
+            for c in range(n):
+                raw[(name, c0 + c)] = piece[:, :, 256 * c : 256 * (c + 1)]
 
         warm = keep.tile([P, 1], F32, name="warm")
         nc.vector.memset(warm[:], 0.0)
@@ -96,7 +98,7 @@ def tile_mix_mel_norm_kernel(tc, x, co, si, gn, fb_words, fb_scales, mu, isd, ou
 
         def cast_permuted(engine, src_tile, grouped, c, m0, m1):
             dst = grouped[:].rearrange("p (j m k) -> p m k j", j=PACK, k=PACK)[:, 64 * c + m0 : 64 * c + m1]
-            src = src_tile[:].rearrange("p k (m j) -> p m k j", j=PACK)[:, m0:m1]
+            src = src_tile.rearrange("p k (m j) -> p m k j", j=PACK)[:, m0:m1]
             copy_on(engine, dst, src)
 
         def grouped_tile(width, name):
@@ -117,7 +119,7 @@ def tile_mix_mel_norm_kernel(tc, x, co, si, gn, fb_words, fb_scales, mu, isd, ou
             return work.tile([P, 2, PACK, P], F32, name="sq%d" % s, tag="sq%d" % s, bufs=4, align_bytes=64)
 
         def square_chunk(s, c, pair):
-            acc = bank("mm", 5)
+            acc = bank("mm", 4)
             fc = slice(256 * c, 256 * (c + 1))
             for i in range(2):
                 cols = slice((2 * pair + i) * P, (2 * pair + i + 1) * P)
@@ -128,7 +130,7 @@ def tile_mix_mel_norm_kernel(tc, x, co, si, gn, fb_words, fb_scales, mu, isd, ou
 
         def square_by_frames(s, a, tt):
             cols = slice(tt * P, (tt + 1) * P)
-            acc = bank("mm", 5)
+            acc = bank("mm", 4)
             mx(acc[:], x_code[:, cols], x_scale[:, cols], w_code[s][a][:], w_scale[s][a][:])
             if tt % 2 == 0:
                 sq_t[(s, a, tt // 2)] = sq_tile(s)
@@ -137,17 +139,21 @@ def tile_mix_mel_norm_kernel(tc, x, co, si, gn, fb_words, fb_scales, mu, isd, ou
 
         power = {}
 
-        def transpose_add(a, tt):
-            acc = bank("tr", 3)
+        def transpose_part(s, a, tt):
+            if s == 0:
+                power[(a, tt)] = bank("tr", 4)
+            acc = power[(a, tt)]
             for j in range(PACK):
-                for s in range(2):
-                    nc.tensor.matmul(out=acc[:, j * P : (j + 1) * P], lhsT=sq_t[(s, a, tt // 2)][:, tt % 2, j, :], rhs=ident[:], start=(s == 0), stop=(s == 1), is_transpose=True)
-            power[(a, tt)] = acc
+                nc.tensor.matmul(out=acc[:, j * P : (j + 1) * P], lhsT=sq_t[(s, a, tt // 2)][:, tt % 2, j, :], rhs=ident[:], start=(s == 0 and j == 0), stop=(s == 1 and j == PACK - 1), is_transpose=True)
+
+        def transpose_add(a, tt):
+            transpose_part(0, a, tt)
+            transpose_part(1, a, tt)
 
         h_val = {}
 
         def h_tile(key):
-            h_val[key] = work.tile([P, 256 * PACK], BF16, name="hv", tag="hv", bufs=4, align_bytes=64)
+            h_val[key] = work.tile([P, 256 * PACK], BF16, name="hv", tag="hv", bufs=5, align_bytes=64)
             return h_val[key]
 
         def apply_gain(a, tt):
@@ -175,7 +181,7 @@ def tile_mix_mel_norm_kernel(tc, x, co, si, gn, fb_words, fb_scales, mu, isd, ou
             sq = keep.tile([P, PACK, width], F32, name="sqf%d_%d" % (s, t0), align_bytes=64)
             per_bank = HALF // width
             for b in range(PACK // per_bank):
-                acc = bank("mm", 5)
+                acc = bank("mm", 4)
                 for i in range(per_bank):
                     j = b * per_bank + i
                     jc = slice(j * P, (j + 1) * P)
@@ -208,7 +214,7 @@ def tile_mix_mel_norm_kernel(tc, x, co, si, gn, fb_words, fb_scales, mu, isd, ou
             )
 
         def filter_bank(t0, width, n_cols):
-            acc = bank("mm", 5)
+            acc = bank("mm", 4)
             for c0 in range(0, width, n_cols):
                 cols = slice(t0 + c0, t0 + c0 + n_cols)
                 for a in range(2):
@@ -230,89 +236,105 @@ def tile_mix_mel_norm_kernel(tc, x, co, si, gn, fb_words, fb_scales, mu, isd, ou
         def quantize_w1(s):
             quantize(w_code[s][1][:], w_scale[s][1][:], g_w1[s][:])
 
+        warm_bank = bank("tr", 4)
+
         def warm_up(n):
-            acc = bank("tr", 3)
+            acc = warm_bank
             for i in range(n):
                 mx(acc[:, 0:256], x_code[:, 0:P], x_scale[:, 0:P], x_code[:, 0:256], x_scale[:, 0:256])
 
+        def sqf(s, pair, n=1):
+            square_by_freq(s, 256 * pair, 256 * n)
         def sq(a, tts):
             for tt in tts:
                 for s in range(2):
                     square_by_frames(s, a, tt)
-        def cast_x(i):
-            cast("v", raw[("x", i)], g_x[i], 0, 256)
-        def prep_x(i):
-            cast_x(i)
-            quantize_x(i)
-        def prep_w(s, c):
-            cast("v", raw[(("co", "si")[s], c)], g_w0[s][c], 0, 256)
-            quantize_w0(s, c)
-        def cast_w1(s, c, e="v"):
-            cast_permuted(e, raw[(("co", "si")[s], 2 + c)], g_w1[s], c, 0, 64)
+        def cast_x(i, e="v", c0=0, c1=256):
+            cast(e, raw[("x", i)], g_x[i], c0, c1)
+        def cast_w0(s, c, e="v", c0=0, c1=256):
+            cast(e, raw[(("co", "si")[s], c)], g_w0[s][c], c0, c1)
+        def cast_w1(s, c, e="v", m0=0, m1=64):
+            cast_permuted(e, raw[(("co", "si")[s], 2 + c)], g_w1[s], c, m0, m1)
         tadd = transpose_add
         gain_ = apply_gain
-        prep_x(0)
-        warm_up(4)
-        prep_w(0, 0)
-        square_chunk(0, 0, 0)
-        warm_up(3)
-        prep_x(1)
-        square_chunk(0, 0, 1)
+        tp = transpose_part
+        cast_x(1, "s")
+        cast_x(0)
+        quantize_x(0)
+        warm_up(8)
+        quantize_x(1)
+        cast_w0(0, 1, "s", 0, 160)
+        cast_w0(0, 0)
+        cast_w0(0, 1, "v", 160, 256)
+        quantize_w0(0, 0)
+        quantize_w0(0, 1)
+        for tt in range(4):
+            square_by_frames(0, 0, tt)
+        cast_w0(1, 0)
+        quantize_w0(1, 0)
         warm_up(2)
-        for s, c in ((0, 1), (1, 0), (1, 1)):
-            prep_w(s, c)
-            square_chunk(s, c, 0)
-            square_chunk(s, c, 1)
-        prep_x(2)
+        tp(0, 0, 0)
+        square_chunk(1, 0, 0)
+        square_chunk(1, 0, 1)
+        cast_w0(1, 1)
+        quantize_w0(1, 1)
+        tp(0, 0, 1)
+        tp(0, 0, 2)
+        square_chunk(1, 1, 0)
+        square_chunk(1, 1, 1)
+        cast_x(2)
+        quantize_x(2)
+        cast_x(3)
         sq(0, (4, 5))
-        tadd(0, 0)
-        cast_w1(0, 0)
-        prep_x(3)
-        gain_(0, 0)
-        tadd(0, 1)
+        quantize_x(3)
+        tp(1, 0, 0)
+        tp(1, 0, 1)
         sq(0, (6, 7))
+        cast_w1(0, 0)
         cast_w1(0, 1)
-        gain_(0, 1)
+        gain_(0, 0)
         quantize_w1(0)
-        tadd(0, 2)
-        tadd(0, 3)
-        cast_w1(1, 0, "v")
-        quantize_h(0, 0)
-        gain_(0, 2)
-        cast_w1(1, 1)
-        square_by_freq(0, 0, 256)
-        square_by_freq(0, 256, 256)
-        gain_(0, 3)
+        tp(0, 0, 3)
+        tp(1, 0, 2)
+        tp(1, 0, 3)
+        sqf(0, 0)
+        cast_w1(1, 0)
+        cast_w1(1, 1, "v", 0, 64)
+        gain_(0, 1)
         quantize_w1(1)
         tadd(0, 4)
+        sqf(1, 0)
+        gain_(0, 2)
+        quantize_h(0, 0)
+        gain_(0, 3)
         tadd(0, 5)
-        quantize_h(0, 1)
-        gain_(0, 4)
-        gain_(0, 5)
-        square_by_freq(1, 0, 256)
-        square_by_freq(1, 256, 256)
         tadd(0, 6)
-        tadd(0, 7)
-        quantize_h(0, 2)
+        sq(1, (2, 3))
+        gain_(0, 4)
+        quantize_h(0, 1)
+        gain_(0, 5)
         add_parts(0)
+        tadd(0, 7)
+        sqf(0, 2)
+        sqf(1, 2)
+        quantize_h(0, 2)
         gain_(0, 6)
         sign_parts(0)
         gain_(0, 7)
         quantize_h(1, 0)
-        sq(1, (4, 5))
-        add_parts(1)
+        tadd(1, 2)
+        tadd(1, 3)
+        sq(1, (6, 7))
         quantize_h(0, 3)
-        sign_parts(1)
-        sq(1, (6,))
-        tadd(1, 4)
-        sq(1, (7,))
-        tadd(1, 5)
-        gain_(1, 4)
+        gain_(1, 2)
+        gain_(1, 3)
+        filter_bank(0, 256, P)
+        add_parts(2)
         quantize_h(1, 1)
-        gain_(1, 5)
         tadd(1, 6)
-        filter_bank(0, HALF, HALF)
+        sign_parts(2)
         tadd(1, 7)
+        filter_bank(256, 256, P)
         gain_(1, 6)
         quantize_h(1, 2)
         gain_(1, 7)

@@ -285,13 +285,16 @@ def tile_mix_mel_norm_kernel(tc, x, co, si, gn, fb_words, fb_scales, mu, isd, ou
         cast_x(2)
         quantize_x(2)
         cast_x(3)
-        sq(0, (4, 5))
+        sq(0, (4,))
+        sq(0, (5,))
         quantize_x(3)
         tp(1, 0, 0)
         tp(1, 0, 1)
-        sq(0, (6, 7))
+        sq(0, (6,))
+        cast_w1(1, 1, "s", 0, 32)
+        sq(0, (7,))
         cast_w1(0, 0)
-        cast_w1(0, 1)
+        cast_w1(0, 1, "v", 0, 64)
         gain_(0, 0)
         quantize_w1(0)
         tp(0, 0, 3)
@@ -299,7 +302,7 @@ def tile_mix_mel_norm_kernel(tc, x, co, si, gn, fb_words, fb_scales, mu, isd, ou
         tp(1, 0, 3)
         sqf(0, 0)
         cast_w1(1, 0)
-        cast_w1(1, 1, "v", 0, 64)
+        cast_w1(1, 1, "v", 32, 64)
         gain_(0, 1)
         quantize_w1(1)
         tadd(0, 4)
@@ -308,29 +311,28 @@ def tile_mix_mel_norm_kernel(tc, x, co, si, gn, fb_words, fb_scales, mu, isd, ou
         quantize_h(0, 0)
         gain_(0, 3)
         tadd(0, 5)
-        tadd(0, 6)
-        sq(1, (2, 3))
+        sqf(0, 1)
+        sqf(1, 1)
         gain_(0, 4)
         quantize_h(0, 1)
         gain_(0, 5)
         add_parts(0)
-        tadd(0, 7)
-        sqf(0, 2)
-        sqf(1, 2)
         quantize_h(0, 2)
-        gain_(0, 6)
         sign_parts(0)
-        gain_(0, 7)
+        tadd(0, 6)
+        sqf(0, 2)
+        tadd(0, 7)
+        sqf(1, 2)
+        gain_(0, 6)
         quantize_h(1, 0)
-        tadd(1, 2)
-        tadd(1, 3)
+        add_parts(1)
+        gain_(0, 7)
+        sign_parts(1)
         sq(1, (6, 7))
         quantize_h(0, 3)
-        gain_(1, 2)
-        gain_(1, 3)
-        filter_bank(0, 256, P)
         add_parts(2)
         quantize_h(1, 1)
+        filter_bank(0, 256, P)
         tadd(1, 6)
         sign_parts(2)
         tadd(1, 7)

from contextlib import ExitStack

import concourse.mybir as mybir
from concourse.masks import make_identity

K, F, N, T = 512, 1024, 128, 1024
FLOPS = 2 * 2 * K * F * T + 2 * F * N * T

F32 = mybir.dt.float32
BF16 = mybir.dt.bfloat16
U32 = mybir.dt.uint32
I32 = mybir.dt.int32
U8 = mybir.dt.uint8
FP8X4 = mybir.dt.float8_e4m3fn_x4
FP4X4 = mybir.dt.float4_e2m1fn_x4
ALU = mybir.AluOpType
ACT = mybir.ActivationFunctionType

P = 128
PACK = 4
HALF = 512


def tile_mix_mel_norm_kernel(tc, x, co, si, gn, fb_words, fb_scales, mu, isd, out):
    nc = tc.nc
    with ExitStack() as ctx:
        keep = ctx.enter_context(tc.tile_pool(name="keep", bufs=1))
        work = ctx.enter_context(tc.tile_pool(name="work", bufs=1))
        psum = ctx.enter_context(tc.psum_pool(name="psum", bufs=1))
        ctx.enter_context(tc.manual_schedule())

        gain = keep.tile([P, 2, PACK], F32, name="gain")
        nc.scalar.dma_start(out=gain[:], in_=gn.rearrange("(a p j) -> p a j", a=2, j=PACK))

        def load(src, c0, width, name):
            raw = keep.tile([P, PACK, width], F32, name=name, align_bytes=64)
            nc.sync.dma_start(out=raw[:], in_=src[:, c0 : c0 + width].rearrange("(p j) w -> p j w", j=PACK))
            return raw

        raw = {}
        for name, c0, n in (("x", 0, 2), ("co", 0, 2), ("si", 0, 2), ("x", 2, 2), ("co", 2, 2), ("si", 2, 2)):
            piece = load({"x": x, "co": co, "si": si}[name], 256 * c0, 256 * n, "%s%d" % (name, c0))
            for c in range(n):
                raw[(name, c0 + c)] = piece[:, :, 256 * c : 256 * (c + 1)]

        warm = keep.tile([P, 1], F32, name="warm")
        nc.vector.memset(warm[:], 0.0)
        warm_out = keep.tile([P, 1], F32, name="warm_out")
        nc.scalar.activation(out=warm_out[:], in_=warm[:], func=ACT.Square)

        fb_scale = keep.tile([P, 2, N], U8, name="fb_scale", align_bytes=64)
        nc.gpsimd.memset(fb_scale[:].bitcast(I32), 0)
        ident = keep.tile([P, P], F32, name="ident", align_bytes=64)
        half = keep.tile([P, PACK], F32, name="half")
        nc.gpsimd.memset(half[:], 0.5)
        make_identity(nc, ident[:])

        is_pos = keep.tile([P, PACK], F32, name="is_pos")
        nc.gpsimd.tensor_scalar(out=is_pos[:], in0=gain[:, 1, :], scalar1=0.0, scalar2=2.0, op0=ALU.is_ge, op1=ALU.mult)
        sgn = keep.tile([P, PACK], F32, name="sgn")
        nc.gpsimd.tensor_scalar(out=sgn[:], in0=is_pos[:], scalar1=1.0, scalar2=-1.0, op0=ALU.mult, op1=ALU.add)
        mag = keep.tile([P, PACK], F32, name="mag")
        nc.gpsimd.tensor_tensor(out=mag[:], in0=gain[:, 1, :], in1=sgn[:], op=ALU.mult)
        root = keep.tile([P, PACK], F32, name="root")
        nc.gpsimd.tensor_tensor(out=root[:], in0=mag[:], in1=half[:], op=ALU.pow)
        sgn_rep = keep.tile([P, 16, PACK], BF16, name="sgn_rep", align_bytes=64)
        nc.gpsimd.tensor_copy(out=sgn_rep[:], in_=sgn[:].unsqueeze(1).to_broadcast([P, 16, PACK]))

        fb_code = keep.tile([P, 2, 2 * N], U8, name="fb_code", align_bytes=64)
        nc.sync.dma_start(out=fb_code[:], in_=fb_words.rearrange("a p b -> p a b"))
        scale_rows = fb_scales.rearrange("a (q r) n -> r q a n", r=4)
        for r in range(4):
            nc.sync.dma_start(out=fb_scale[r:P:32].bitcast(I32), in_=scale_rows[r].bitcast(I32))
        mean = keep.tile([P, 1], F32, name="mean")
        nc.sync.dma_start(out=mean[:], in_=mu.rearrange("(p o) -> p o", o=1))
        inv_dev = keep.tile([P, 1], F32, name="inv_dev")
        nc.sync.dma_start(out=inv_dev[:], in_=isd.rearrange("(p o) -> p o", o=1))
        shift = keep.tile([P, 1], F32, name="shift")
        nc.gpsimd.tensor_scalar(out=shift[:], in0=mean[:], scalar1=inv_dev[:], scalar2=-1.0, op0=ALU.mult, op1=ALU.mult)

        x_code = keep.tile([P, T], U32, name="x_code", align_bytes=64)
        x_scale = keep.tile([P, T], U8, name="x_scale", align_bytes=64)
        w_code = [[keep.tile([P, HALF], U32, name="wc%d%d" % (s, a), align_bytes=64) for a in range(2)] for s in range(2)]
        w_scale = [[keep.tile([P, HALF], U8, name="ws%d%d" % (s, a), align_bytes=64) for a in range(2)] for s in range(2)]
        h_code = [keep.tile([P, T], U32, name="hc%d" % a, align_bytes=64) for a in range(2)]
        h_scale = [keep.tile([P, T], U8, name="hs%d" % a, align_bytes=64) for a in range(2)]

        def copy_on(engine, dst, src):
            if engine == "v":
                nc.vector.tensor_copy(out=dst, in_=src)
            else:
                nc.scalar.copy(out=dst, in_=src)

        def cast(engine, raw, grouped, c0, c1):
            dst = grouped[:].rearrange("p (w k) -> p w k", k=PACK)[:, c0:c1, :].rearrange("p (c i) k -> p c k i", i=4)
            src = raw[:, :, c0:c1].rearrange("p k (c i) -> p c k i", i=4)
            copy_on(engine, dst, src)

        def cast_permuted(engine, src_tile, grouped, c, m0, m1):
            dst = grouped[:].rearrange("p (j m k) -> p m k j", j=PACK, k=PACK)[:, 64 * c + m0 : 64 * c + m1]
            src = src_tile.rearrange("p k (m j) -> p m k j", j=PACK)[:, m0:m1]
            copy_on(engine, dst, src)

        def grouped_tile(width, name):
            return keep.tile([P, width * PACK], BF16, name=name, align_bytes=64)

        def quantize(codes, scales, values):
            nc.vector.quantize_mx(out=codes.bitcast(FP8X4), scales=scales, in_=values)

        def mx(dst, lc, ls, rc, rs, start=True, stop=True, ldt=FP8X4):
            nc.tensor.matmul_mx(out=dst, lhsT=lc.bitcast(ldt), lhsT_scale=ls, rhs=rc.bitcast(FP8X4), rhs_scale=rs, start=start, stop=stop)

        def bank(tag, bufs):
            return psum.tile([P, HALF], F32, name=tag, tag=tag, bufs=bufs)

        sq_t = {}

        def sq_tile(s):
            return work.tile([P, 2, PACK, P], F32, name="sq%d" % s, tag="sq%d" % s, bufs=4, align_bytes=64)

        def square_chunk(s, c, pair):
            acc = bank("mm", 4)
            fc = slice(256 * c, 256 * (c + 1))
            for i in range(2):
                cols = slice((2 * pair + i) * P, (2 * pair + i + 1) * P)
                mx(acc[:, 256 * i : 256 * (i + 1)], x_code[:, cols], x_scale[:, cols], w_code[s][0][:, fc], w_scale[s][0][:, fc])
            if c == 0:
                sq_t[(s, 0, pair)] = sq_tile(s)
            nc.scalar.activation(out=sq_t[(s, 0, pair)][:, :, :, 64 * c : 64 * (c + 1)], in_=acc[:].rearrange("t (i m j) -> t i j m", i=2, j=PACK), func=ACT.Square)

        def square_by_frames(s, a, tt):
            cols = slice(tt * P, (tt + 1) * P)
            acc = bank("mm", 4)
            mx(acc[:], x_code[:, cols], x_scale[:, cols], w_code[s][a][:], w_scale[s][a][:])
            if tt % 2 == 0:
                sq_t[(s, a, tt // 2)] = sq_tile(s)
            order = "t (m j) -> t j m" if a == 0 else "t (j m) -> t j m"
            nc.scalar.activation(out=sq_t[(s, a, tt // 2)][:, tt % 2], in_=acc[:].rearrange(order, j=PACK), func=ACT.Square)

        power = {}

        def transpose_part(s, a, tt):
            if s == 0:
                power[(a, tt)] = bank("tr", 4)
            acc = power[(a, tt)]
            for j in range(PACK):
                nc.tensor.matmul(out=acc[:, j * P : (j + 1) * P], lhsT=sq_t[(s, a, tt // 2)][:, tt % 2, j, :], rhs=ident[:], start=(s == 0 and j == 0), stop=(s == 1 and j == PACK - 1), is_transpose=True)

        def transpose_add(a, tt):
            transpose_part(0, a, tt)
            transpose_part(1, a, tt)

        h_val = {}

        def h_tile(key):
            h_val[key] = work.tile([P, 256 * PACK], BF16, name="hv", tag="hv", bufs=5, align_bytes=64)
            return h_val[key]

        def apply_gain(a, tt):
            hv = h_tile((a, tt // 2)) if tt % 2 == 0 else h_val[(a, tt // 2)]
            i = tt % 2
            nc.vector.tensor_tensor(
                out=hv[:, i * HALF : (i + 1) * HALF].rearrange("p (t j) -> p t j", j=PACK),
                in0=power[(a, tt)][:].rearrange("p (j t) -> p t j", j=PACK),
                in1=gain[:, a, :].unsqueeze(1).to_broadcast([P, P, PACK]),
                op=ALU.mult,
            )

        def quantize_h(a, pair):
            cols = slice(256 * pair, 256 * (pair + 1))
            quantize(h_code[a][:, cols], h_scale[a][:, cols], h_val[(a, pair)][:])

        def quantize_h1(a, tt):
            cols = slice(P * tt, P * (tt + 1))
            i = tt % 2
            quantize(h_code[a][:, cols], h_scale[a][:, cols], h_val[(a, tt // 2)][:, i * HALF : (i + 1) * HALF])
        sq_f = {}

        def square_by_freq(s, t0, width):
            cols = slice(t0, t0 + width)
            sq = keep.tile([P, PACK, width], F32, name="sqf%d_%d" % (s, t0), align_bytes=64)
            per_bank = HALF // width
            for b in range(PACK // per_bank):
                acc = bank("mm", 4)
                for i in range(per_bank):
                    j = b * per_bank + i
                    jc = slice(j * P, (j + 1) * P)
                    mx(acc[:, i * width : (i + 1) * width], w_code[s][1][:, jc], w_scale[s][1][:, jc], x_code[:, cols], x_scale[:, cols])
                for i in range(per_bank):
                    j = b * per_bank + i
                    nc.scalar.activation(out=sq[:, j, :], in_=acc[:, i * width : (i + 1) * width], func=ACT.Square, scale=root[:, j : j + 1])
            for q in range(width // 256):
                sq_f[(s, t0 // 256 + q)] = sq[:, :, 256 * q : 256 * (q + 1)]

        h_abs = {}

        def add_parts(pair):
            ha = work.tile([P, 256 * PACK], BF16, name="ha", tag="ha", bufs=2, align_bytes=64)
            nc.vector.tensor_tensor(
                out=ha[:].rearrange("p (c i j) -> p c j i", i=4, j=PACK),
                in0=sq_f[(0, pair)].rearrange("p j (c i) -> p c j i", i=4),
                in1=sq_f[(1, pair)].rearrange("p j (c i) -> p c j i", i=4),
                op=ALU.add,
            )
            h_abs[pair] = ha

        def sign_parts(pair):
            hv = h_tile((1, pair))
            nc.vector.tensor_tensor(
                out=hv[:].rearrange("p (r e) -> p r e", e=64),
                in0=h_abs[pair][:].rearrange("p (r e) -> p r e", e=64),
                in1=sgn_rep[:].rearrange("p r j -> p (r j)").unsqueeze(1).to_broadcast([P, 16, 64]),
                op=ALU.mult,
            )

        def filter_bank(t0, width, n_cols):
            acc = bank("mm", 4)
            for c0 in range(0, width, n_cols):
                cols = slice(t0 + c0, t0 + c0 + n_cols)
                for a in range(2):
                    mx(acc[:, c0 : c0 + n_cols], fb_code[:, a, :], fb_scale[:, a, :], h_code[a][:, cols], h_scale[a][:, cols], start=(a == 0), stop=(a == 1), ldt=FP4X4)
            res = keep.tile([P, width], F32, name="res%d" % t0, align_bytes=64)
            nc.scalar.activation(out=res[:], in_=acc[:, 0:width], func=ACT.Identity, scale=inv_dev[:], bias=shift[:])
            nc.sync.dma_start(out=out[:, t0 : t0 + width], in_=res[:])

        g_x = [grouped_tile(256, "g_x%d" % i) for i in range(4)]
        g_w0 = [[grouped_tile(256, "g_w0_%d%d" % (s, c)) for c in range(2)] for s in range(2)]
        g_w1 = [grouped_tile(HALF, "g_w1_%d" % s) for s in range(2)]

        def quantize_x(i):
            quantize(x_code[:, 256 * i : 256 * (i + 1)], x_scale[:, 256 * i : 256 * (i + 1)], g_x[i][:])

        def quantize_w0(s, c):
            quantize(w_code[s][0][:, 256 * c : 256 * (c + 1)], w_scale[s][0][:, 256 * c : 256 * (c + 1)], g_w0[s][c][:])

        def quantize_w1(s):
            quantize(w_code[s][1][:], w_scale[s][1][:], g_w1[s][:])

        warm_bank = bank("tr", 4)

        def warm_up(n):
            acc = warm_bank
            for i in range(n):
                mx(acc[:, 0:256], x_code[:, 0:P], x_scale[:, 0:P], x_code[:, 0:256], x_scale[:, 0:256])

        def sqf(s, pair, n=1):
            square_by_freq(s, 256 * pair, 256 * n)
        def sq(a, tts):
            for tt in tts:
                for s in range(2):
                    square_by_frames(s, a, tt)
        def cast_x(i, e="v", c0=0, c1=256):
            cast(e, raw[("x", i)], g_x[i], c0, c1)
        def cast_w0(s, c, e="v", c0=0, c1=256):
            cast(e, raw[(("co", "si")[s], c)], g_w0[s][c], c0, c1)
        def cast_w1(s, c, e="v", m0=0, m1=64):
            cast_permuted(e, raw[(("co", "si")[s], 2 + c)], g_w1[s], c, m0, m1)
        tadd = transpose_add
        gain_ = apply_gain
        tp = transpose_part
        cast_x(1, "s")
        cast_x(0)
        quantize_x(0)
        warm_up(8)
        quantize_x(1)
        cast_w0(0, 1, "s", 0, 160)
        cast_w0(0, 0)
        cast_w0(0, 1, "v", 160, 256)
        quantize_w0(0, 0)
        quantize_w0(0, 1)
        for tt in range(4):
            square_by_frames(0, 0, tt)
        cast_w0(1, 0)
        quantize_w0(1, 0)
        warm_up(2)
        tp(0, 0, 0)
        square_chunk(1, 0, 0)
        square_chunk(1, 0, 1)
        cast_w0(1, 1)
        quantize_w0(1, 1)
        tp(0, 0, 1)
        tp(0, 0, 2)
        square_chunk(1, 1, 0)
        square_chunk(1, 1, 1)
        cast_x(2)
        quantize_x(2)
        cast_x(3)
        sq(0, (4,))
        sq(0, (5,))
        quantize_x(3)
        tp(1, 0, 0)
        tp(1, 0, 1)
        sq(0, (6,))
        cast_w1(1, 1, "s", 0, 32)
        sq(0, (7,))
        cast_w1(0, 0)
        cast_w1(0, 1, "v", 0, 64)
        gain_(0, 0)
        quantize_w1(0)
        tp(0, 0, 3)
        tp(1, 0, 2)
        tp(1, 0, 3)
        sqf(0, 0)
        cast_w1(1, 0)
        cast_w1(1, 1, "v", 32, 64)
        gain_(0, 1)
        quantize_w1(1)
        tadd(0, 4)
        sqf(1, 0)
        gain_(0, 2)
        quantize_h(0, 0)
        gain_(0, 3)
        tadd(0, 5)
        sqf(0, 1)
        sqf(1, 1)
        gain_(0, 4)
        quantize_h(0, 1)
        gain_(0, 5)
        add_parts(0)
        quantize_h(0, 2)
        sign_parts(0)
        tadd(0, 6)
        sqf(0, 2)
        tadd(0, 7)
        sqf(1, 2)
        gain_(0, 6)
        quantize_h(1, 0)
        add_parts(1)
        gain_(0, 7)
        sign_parts(1)
        sq(1, (6, 7))
        quantize_h(0, 3)
        add_parts(2)
        quantize_h(1, 1)
        filter_bank(0, 256, P)
        tadd(1, 6)
        sign_parts(2)
        tadd(1, 7)
        filter_bank(256, 256, P)
        gain_(1, 6)
        quantize_h(1, 2)
        gain_(1, 7)
        quantize_h1(1, 6)
        quantize_h1(1, 7)
        filter_bank(512, 256, P)
        filter_bank(768, P, P)
        filter_bank(896, P, P)
